import numpy as np
CORES = [11,27,43,59,75,91,107,123]
N = 8
ROOT = 5
def setup_inputs(rng):
    return {"x": rng.standard_normal((N, 128, 256), dtype=np.float32)}
def reference(x):
    y = np.full((N, 128, N * 256), np.nan, x.dtype)
    y[ROOT] = np.concatenate(list(x), axis=1)
    return {"y": y}

@@ -1,0 +1,67 @@
+SCRATCH = {
+    "stage": ("dram", [128, 256], "float32"),
+    "hop": ("dram", [128, 256], "float32"),
+    "land": ("sbuf", [128, 2048], "float32"),
+}
+SEMAPHORES = ["loaded", "sent", "hopin", "arrA", "arrD", "arrM", "stored"]
+
+W = 256
+WAY_A = (0, 1, 2)
+WAY_D = (3, 4)
+WAY_M = (6, 7)
+M_RELAY_CORE = {6: 3, 7: 7}
+D_HELPER_CORE = 4
+
+
+def rank_program(g, core, T, topo):
+    root = T.cores[5]
+    root_chip = topo.chip(root)
+    mate_chip = root_chip ^ 1
+
+    def send(dst, out_ap, in_ap, remote_sem):
+        rid, pid, _se = topo.addr(dst)
+        m = topo.mask(core, dst)
+        g.remote_dma(out_ap, in_ap, remote_sem, T.sem.sent, pid, rid, m)
+        return 16 if m == 0xFFFF else 8
+
+    helpers = {}
+    for r in WAY_D:
+        helpers[topo.chip(T.cores[r]) * 8 + D_HELPER_CORE] = (r, 16, T.sem.arrD)
+    for r in WAY_M:
+        helpers[mate_chip * 8 + M_RELAY_CORE[r]] = (r, 8, T.sem.arrM)
+
+    rank = T.rank_of(core)
+
+    if core in helpers:
+        r, n_in, arr = helpers[core]
+        g.wait_ge(T.sem.hopin, n_in)
+        n = send(root, T.land[:, W * r:W * (r + 1)], T.hop[:], arr)
+        g.wait_ge(T.sem.sent, n)
+        return
+
+    if rank is None:
+        return
+
+    if core == root:
+        g.scalar.dma_start(T.y[:, W * rank:W * (rank + 1)], T.x[:]).then_inc(T.sem.stored, 16)
+        a0, a1 = W * WAY_A[0], W * (WAY_A[-1] + 1)
+        g.sync.wait_ge(T.sem.arrA, 8 * len(WAY_A))
+        g.sync.dma_start(T.y[:, a0:a1], T.land[:, a0:a1]).then_inc(T.sem.stored, 16)
+        d0, d1 = W * WAY_D[0], W * (WAY_D[-1] + 1)
+        g.scalar.wait_ge(T.sem.arrD, 8 * len(WAY_D))
+        g.scalar.dma_start(T.y[:, d0:d1], T.land[:, d0:d1]).then_inc(T.sem.stored, 16)
+        m0, m1 = W * WAY_M[0], W * (WAY_M[-1] + 1)
+        g.sync.wait_ge(T.sem.arrM, 8 * len(WAY_M))
+        g.sync.dma_start(T.y[:, m0:m1], T.land[:, m0:m1]).then_inc(T.sem.stored, 16)
+        g.wait_ge(T.sem.stored, 64)
+        return
+
+    g.sync.dma_start(T.stage[:], T.x[:]).then_inc(T.sem.loaded, 16)
+    g.wait_ge(T.sem.loaded, 16)
+    if rank in WAY_A:
+        n = send(root, T.land[:, W * rank:W * (rank + 1)], T.stage[:], T.sem.arrA)
+    elif rank in WAY_D:
+        n = send(topo.chip(core) * 8 + D_HELPER_CORE, T.hop[:], T.stage[:], T.sem.hopin)
+    else:
+        n = send(mate_chip * 8 + M_RELAY_CORE[rank], T.hop[:], T.stage[:], T.sem.hopin)
+    g.wait_ge(T.sem.sent, n)

@@ -1,67 +1,72 @@
-SCRATCH = {
-    "stage": ("dram", [128, 256], "float32"),
-    "hop": ("dram", [128, 256], "float32"),
-    "land": ("sbuf", [128, 2048], "float32"),
-}
-SEMAPHORES = ["loaded", "sent", "hopin", "arrA", "arrD", "arrM", "stored"]
-
 W = 256
-WAY_A = (0, 1, 2)
-WAY_D = (3, 4)
-WAY_M = (6, 7)
-M_RELAY_CORE = {6: 3, 7: 7}
-D_HELPER_CORE = 4
+PIECES = [
+    (0, 0, 128, ("A",)),
+    (1, 0, 128, ("A",)),
+    (2, 0, 128, ("A",)),
+    (3, 0, 128, ("D", 4)),
+    (4, 0, 128, ("D", 4)),
+    (6, 0, 96, ("M", 3)),
+    (6, 96, 32, ("A",)),
+    (7, 0, 96, ("M", 7)),
+    (7, 96, 32, ("D", 4)),
+]
+STORES = {"sync": [0, 2, 6, 3, 5], "scalar": [1, 4, 8, 7]}
+
+SCRATCH = {}
+for _i, _p in enumerate(PIECES):
+    SCRATCH["p%d" % _i] = ("dram", [128, 2 * _p[2]], "float32")
+SEMAPHORES = ["l0", "l1", "sent", "hopin", "stored"] + ["a%d" % _i for _i in range(len(PIECES))]
 
 
 def rank_program(g, core, T, topo):
     root = T.cores[5]
-    root_chip = topo.chip(root)
-    mate_chip = root_chip ^ 1
+    mate_chip = topo.chip(root) ^ 1
 
-    def send(dst, out_ap, in_ap, remote_sem):
+    def send(dst, buf, remote_sem):
         rid, pid, _se = topo.addr(dst)
         m = topo.mask(core, dst)
-        g.remote_dma(out_ap, in_ap, remote_sem, T.sem.sent, pid, rid, m)
+        g.remote_dma(buf[:], buf[:], remote_sem, T.sem.sent, pid, rid, m)
         return 16 if m == 0xFFFF else 8
 
-    helpers = {}
-    for r in WAY_D:
-        helpers[topo.chip(T.cores[r]) * 8 + D_HELPER_CORE] = (r, 16, T.sem.arrD)
-    for r in WAY_M:
-        helpers[mate_chip * 8 + M_RELAY_CORE[r]] = (r, 8, T.sem.arrM)
+    def helper_core(i):
+        r, _r0, _n, way = PIECES[i]
+        if way[0] == "A":
+            return None
+        return (topo.chip(T.cores[r]) if way[0] == "D" else mate_chip) * 8 + way[1]
 
     rank = T.rank_of(core)
 
-    if core in helpers:
-        r, n_in, arr = helpers[core]
-        g.wait_ge(T.sem.hopin, n_in)
-        n = send(root, T.land[:, W * r:W * (r + 1)], T.hop[:], arr)
-        g.wait_ge(T.sem.sent, n)
-        return
+    for i in range(len(PIECES)):
+        if helper_core(i) == core:
+            g.wait_ge(T.sem.hopin, 16 if PIECES[i][3][0] == "D" else 8)
+            n = send(root, T["p%d" % i], T.sem["a%d" % i])
+            g.wait_ge(T.sem.sent, n)
+            return
 
     if rank is None:
         return
 
     if core == root:
         g.scalar.dma_start(T.y[:, W * rank:W * (rank + 1)], T.x[:]).then_inc(T.sem.stored, 16)
-        a0, a1 = W * WAY_A[0], W * (WAY_A[-1] + 1)
-        g.sync.wait_ge(T.sem.arrA, 8 * len(WAY_A))
-        g.sync.dma_start(T.y[:, a0:a1], T.land[:, a0:a1]).then_inc(T.sem.stored, 16)
-        d0, d1 = W * WAY_D[0], W * (WAY_D[-1] + 1)
-        g.scalar.wait_ge(T.sem.arrD, 8 * len(WAY_D))
-        g.scalar.dma_start(T.y[:, d0:d1], T.land[:, d0:d1]).then_inc(T.sem.stored, 16)
-        m0, m1 = W * WAY_M[0], W * (WAY_M[-1] + 1)
-        g.sync.wait_ge(T.sem.arrM, 8 * len(WAY_M))
-        g.sync.dma_start(T.y[:, m0:m1], T.land[:, m0:m1]).then_inc(T.sem.stored, 16)
-        g.wait_ge(T.sem.stored, 64)
+        for qn, q in (("sync", g.sync), ("scalar", g.scalar)):
+            for i in STORES[qn]:
+                r, r0, n, _way = PIECES[i]
+                q.wait_ge(T.sem["a%d" % i], 8)
+                q.dma_start(T.y[r0:r0 + n, W * r:W * (r + 1)], T["p%d" % i][:]).then_inc(T.sem.stored, 16)
+        g.wait_ge(T.sem.stored, 16 * (1 + len(PIECES)))
         return
 
-    g.sync.dma_start(T.stage[:], T.x[:]).then_inc(T.sem.loaded, 16)
-    g.wait_ge(T.sem.loaded, 16)
-    if rank in WAY_A:
-        n = send(root, T.land[:, W * rank:W * (rank + 1)], T.stage[:], T.sem.arrA)
-    elif rank in WAY_D:
-        n = send(topo.chip(core) * 8 + D_HELPER_CORE, T.hop[:], T.stage[:], T.sem.hopin)
-    else:
-        n = send(mate_chip * 8 + M_RELAY_CORE[rank], T.hop[:], T.stage[:], T.sem.hopin)
-    g.wait_ge(T.sem.sent, n)
+    mine = [i for i in range(len(PIECES)) if PIECES[i][0] == rank]
+    for k, i in enumerate(mine):
+        _r, r0, n, _way = PIECES[i]
+        q = g.sync if k == 0 else g.scalar
+        q.dma_start(T["p%d" % i][:], T.x[r0:r0 + n, :]).then_inc(T.sem["l%d" % k], 16)
+    total = 0
+    for k, i in enumerate(mine):
+        g.wait_ge(T.sem["l%d" % k], 16)
+        h = helper_core(i)
+        if h is None:
+            total += send(root, T["p%d" % i], T.sem["a%d" % i])
+        else:
+            total += send(h, T["p%d" % i], T.sem.hopin)
+    g.wait_ge(T.sem.sent, total)

@@ -1,72 +1,115 @@
+from concourse.bass import DstId, RemoteDMATransfer
+
 W = 256
-PIECES = [
-    (0, 0, 128, ("A",)),
-    (1, 0, 128, ("A",)),
-    (2, 0, 128, ("A",)),
-    (3, 0, 128, ("D", 4)),
-    (4, 0, 128, ("D", 4)),
-    (6, 0, 96, ("M", 3)),
-    (6, 96, 32, ("A",)),
-    (7, 0, 96, ("M", 7)),
-    (7, 96, 32, ("D", 4)),
-]
-STORES = {"sync": [0, 2, 6, 3, 5], "scalar": [1, 4, 8, 7]}
+WHOLE = {0: ("A",), 1: ("A",), 2: ("A",), 3: ("D", 4), 4: ("D", 4)}
+QUART = {6: [("M", 3), ("M", 3), ("M", 2), ("M", 2)],
+         7: [("M", 7), ("M", 7), ("M", 6), ("D", 4)]}
+STORES = {"sync": [("a", 0), ("a", 2), ("a", 3), ("q", 6), ("m", 6)],
+          "scalar": [("a", 1), ("a", 4), ("q", 7), ("m", 7)]}
 
 SCRATCH = {}
-for _i, _p in enumerate(PIECES):
-    SCRATCH["p%d" % _i] = ("dram", [128, 2 * _p[2]], "float32")
-SEMAPHORES = ["l0", "l1", "sent", "hopin", "stored"] + ["a%d" % _i for _i in range(len(PIECES))]
+for _r in WHOLE:
+    SCRATCH["b%d" % _r] = ("dram", [128, 256], "float32")
+for _r in QUART:
+    SCRATCH["b%d" % _r] = ("dram", [4, 128, 64], "float32")
+SEMAPHORES = (["loaded", "sent", "hopin", "stored"] + ["a%d" % _r for _r in WHOLE]
+              + ["m%d" % _r for _r in QUART] + ["q%d" % _r for _r in QUART])
 
 
 def rank_program(g, core, T, topo):
     root = T.cores[5]
     mate_chip = topo.chip(root) ^ 1
 
-    def send(dst, buf, remote_sem):
-        rid, pid, _se = topo.addr(dst)
-        m = topo.mask(core, dst)
-        g.remote_dma(buf[:], buf[:], remote_sem, T.sem.sent, pid, rid, m)
-        return 16 if m == 0xFFFF else 8
-
-    def helper_core(i):
-        r, _r0, _n, way = PIECES[i]
+    def via(r, way):
         if way[0] == "A":
             return None
         return (topo.chip(T.cores[r]) if way[0] == "D" else mate_chip) * 8 + way[1]
 
+    def xfer(dst, ap, mask, sem):
+        rid, pid, _se = topo.addr(dst)
+        return RemoteDMATransfer(dst_ids=[DstId(rid=rid, pnc=pid)], dma_engine_mask=mask, remote_sem=sem,
+                                 src=ap, dst=ap)
+
+    def bits(lo, n):
+        return ((1 << n) - 1) << lo
+
+    def root_sem(r, s):
+        return ("m%d" if s < 3 else "q%d") % r
+
+    first = {}
+    holds = {}
+    expect = {}
+    for r, ways in QUART.items():
+        lo = 0
+        for s, way in enumerate(ways):
+            h = via(r, way)
+            if h is None:
+                first[(r, s)] = (root, bits(lo, 2), 2, root_sem(r, s))
+                expect[root_sem(r, s)] = expect.get(root_sem(r, s), 0) + 2
+                lo += 2
+                continue
+            holds.setdefault(h, []).append((r, s))
+            if way[0] == "D":
+                first[(r, s)] = (h, 0xFF00, 8, "hopin")
+            else:
+                first[(r, s)] = (h, bits(lo, 2), 2, "hopin")
+                lo += 2
+    for h, got in holds.items():
+        for r, s in got:
+            expect[root_sem(r, s)] = expect.get(root_sem(r, s), 0) + 8 // len(got)
+
     rank = T.rank_of(core)
 
-    for i in range(len(PIECES)):
-        if helper_core(i) == core:
-            g.wait_ge(T.sem.hopin, 16 if PIECES[i][3][0] == "D" else 8)
-            n = send(root, T["p%d" % i], T.sem["a%d" % i])
-            g.wait_ge(T.sem.sent, n)
+    for r, way in WHOLE.items():
+        if via(r, way) == core:
+            g.wait_ge(T.sem.hopin, 16)
+            g.remote_dma_fused([xfer(root, T["b%d" % r][:], 0xFF, T.sem["a%d" % r])], local_sem=T.sem.sent)
+            g.wait_ge(T.sem.sent, 8)
             return
+    if core in holds:
+        got = holds[core]
+        g.wait_ge(T.sem.hopin, sum(first[k][2] for k in got))
+        n = 8 // len(got)
+        g.remote_dma_fused([xfer(root, T["b%d" % r][s], bits(n * j, n), T.sem[root_sem(r, s)])
+                            for j, (r, s) in enumerate(got)], local_sem=T.sem.sent)
+        g.wait_ge(T.sem.sent, 8)
+        return
 
     if rank is None:
         return
 
     if core == root:
         g.scalar.dma_start(T.y[:, W * rank:W * (rank + 1)], T.x[:]).then_inc(T.sem.stored, 16)
+        n_st = 1
         for qn, q in (("sync", g.sync), ("scalar", g.scalar)):
-            for i in STORES[qn]:
-                r, r0, n, _way = PIECES[i]
-                q.wait_ge(T.sem["a%d" % i], 8)
-                q.dma_start(T.y[r0:r0 + n, W * r:W * (r + 1)], T["p%d" % i][:]).then_inc(T.sem.stored, 16)
-        g.wait_ge(T.sem.stored, 16 * (1 + len(PIECES)))
+            for kind, r in STORES[qn]:
+                cols = slice(W * r, W * (r + 1))
+                b = T["b%d" % r]
+                if kind == "a":
+                    q.wait_ge(T.sem["a%d" % r], 8)
+                    q.dma_start(T.y[:, cols], b[:]).then_inc(T.sem.stored, 16)
+                elif kind == "m":
+                    q.wait_ge(T.sem["m%d" % r], expect["m%d" % r])
+                    q.dma_start(T.y[0:96, cols], b[0:3]).then_inc(T.sem.stored, 16)
+                else:
+                    q.wait_ge(T.sem["q%d" % r], expect["q%d" % r])
+                    q.dma_start(T.y[96:128, cols], b[3]).then_inc(T.sem.stored, 16)
+                n_st += 1
+        g.wait_ge(T.sem.stored, 16 * n_st)
         return
 
-    mine = [i for i in range(len(PIECES)) if PIECES[i][0] == rank]
-    for k, i in enumerate(mine):
-        _r, r0, n, _way = PIECES[i]
-        q = g.sync if k == 0 else g.scalar
-        q.dma_start(T["p%d" % i][:], T.x[r0:r0 + n, :]).then_inc(T.sem["l%d" % k], 16)
-    total = 0
-    for k, i in enumerate(mine):
-        g.wait_ge(T.sem["l%d" % k], 16)
-        h = helper_core(i)
+    b = T["b%d" % rank]
+    g.sync.dma_start(b[:], T.x[:]).then_inc(T.sem.loaded, 16)
+    g.wait_ge(T.sem.loaded, 16)
+    if rank in WHOLE:
+        h = via(rank, WHOLE[rank])
         if h is None:
-            total += send(root, T["p%d" % i], T.sem["a%d" % i])
+            g.remote_dma_fused([xfer(root, b[:], 0xFF, T.sem["a%d" % rank])], local_sem=T.sem.sent)
+            g.wait_ge(T.sem.sent, 8)
         else:
-            total += send(h, T["p%d" % i], T.sem.hopin)
-    g.wait_ge(T.sem.sent, total)
+            g.remote_dma_fused([xfer(h, b[:], 0xFFFF, T.sem.hopin)], local_sem=T.sem.sent)
+            g.wait_ge(T.sem.sent, 16)
+    else:
+        fs = [first[(rank, s)] for s in range(4)]
+        g.remote_dma_fused([xfer(f[0], b[s], f[1], T.sem[f[3]]) for s, f in enumerate(fs)], local_sem=T.sem.sent)
+        g.wait_ge(T.sem.sent, sum(f[2] for f in fs))

@@ -1,19 +1,23 @@
 from concourse.bass import DstId, RemoteDMATransfer
 
 W = 256
-WHOLE = {0: ("A",), 1: ("A",), 2: ("A",), 3: ("D", 4), 4: ("D", 4)}
-QUART = {6: [("M", 3), ("M", 3), ("M", 2), ("M", 2)],
-         7: [("M", 7), ("M", 7), ("M", 6), ("D", 4)]}
-STORES = {"sync": [("a", 0), ("a", 2), ("a", 3), ("q", 6), ("m", 6)],
-          "scalar": [("a", 1), ("a", 4), ("q", 7), ("m", 7)]}
+A = ("A",)
+WAYS = {
+    0: [A, A, A, A],
+    1: [A, A, A, A],
+    2: [A, A, A, A],
+    3: [("D", 4), ("D", 4), ("D", 5), ("D", 5)],
+    4: [("D", 4), ("D", 4), ("D", 5), ("D", 5)],
+    6: [("M", 3), ("M", 7), ("M", 2), ("M", 6)],
+    7: [("M", 3), ("M", 7), ("M", 2), ("D", 4)],
+}
+STORES = {"sync": [(0, 0), (2, 0), (4, 0), (7, 0), (0, 1), (2, 1), (4, 1), (7, 1)],
+          "scalar": [(1, 0), (3, 0), (6, 0), (1, 1), (3, 1), (6, 1)]}
 
 SCRATCH = {}
-for _r in WHOLE:
-    SCRATCH["b%d" % _r] = ("dram", [128, 256], "float32")
-for _r in QUART:
+for _r in WAYS:
     SCRATCH["b%d" % _r] = ("dram", [4, 128, 64], "float32")
-SEMAPHORES = (["loaded", "sent", "hopin", "stored"] + ["a%d" % _r for _r in WHOLE]
-              + ["m%d" % _r for _r in QUART] + ["q%d" % _r for _r in QUART])
+SEMAPHORES = ["loaded", "sent", "hopin", "stored"] + ["w%d_%d" % (_r, _w) for _r in WAYS for _w in (0, 1)]
 
 
 def rank_program(g, core, T, topo):
@@ -33,44 +37,40 @@ def rank_program(g, core, T, topo):
     def bits(lo, n):
         return ((1 << n) - 1) << lo
 
-    def root_sem(r, s):
-        return ("m%d" if s < 3 else "q%d") % r
+    def wsem(r, s):
+        return "w%d_%d" % (r, s // 2)
 
     first = {}
     holds = {}
     expect = {}
-    for r, ways in QUART.items():
-        lo = 0
-        for s, way in enumerate(ways):
-            h = via(r, way)
-            if h is None:
-                first[(r, s)] = (root, bits(lo, 2), 2, root_sem(r, s))
-                expect[root_sem(r, s)] = expect.get(root_sem(r, s), 0) + 2
-                lo += 2
-                continue
-            holds.setdefault(h, []).append((r, s))
-            if way[0] == "D":
-                first[(r, s)] = (h, 0xFF00, 8, "hopin")
-            else:
-                first[(r, s)] = (h, bits(lo, 2), 2, "hopin")
-                lo += 2
+    for r, ways in WAYS.items():
+        for w in (0, 1):
+            both_on_chip = ways[2 * w][0] == "D" and ways[2 * w + 1][0] == "D"
+            for j in (0, 1):
+                s = 2 * w + j
+                way = ways[s]
+                h = via(r, way)
+                if way[0] == "D":
+                    mask, n = (bits(8 * j, 8) if both_on_chip else 0xFF00), 8
+                else:
+                    mask, n = bits(4 * j, 4), 4
+                if h is None:
+                    first[(r, s)] = (root, mask, n, wsem(r, s))
+                    expect[wsem(r, s)] = expect.get(wsem(r, s), 0) + n
+                else:
+                    first[(r, s)] = (h, mask, n, "hopin")
+                    holds.setdefault(h, []).append((r, s))
     for h, got in holds.items():
         for r, s in got:
-            expect[root_sem(r, s)] = expect.get(root_sem(r, s), 0) + 8 // len(got)
+            expect[wsem(r, s)] = expect.get(wsem(r, s), 0) + 8 // len(got)
 
     rank = T.rank_of(core)
 
-    for r, way in WHOLE.items():
-        if via(r, way) == core:
-            g.wait_ge(T.sem.hopin, 16)
-            g.remote_dma_fused([xfer(root, T["b%d" % r][:], 0xFF, T.sem["a%d" % r])], local_sem=T.sem.sent)
-            g.wait_ge(T.sem.sent, 8)
-            return
     if core in holds:
         got = holds[core]
         g.wait_ge(T.sem.hopin, sum(first[k][2] for k in got))
         n = 8 // len(got)
-        g.remote_dma_fused([xfer(root, T["b%d" % r][s], bits(n * j, n), T.sem[root_sem(r, s)])
+        g.remote_dma_fused([xfer(root, T["b%d" % r][s], bits(n * j, n), T.sem[wsem(r, s)])
                             for j, (r, s) in enumerate(got)], local_sem=T.sem.sent)
         g.wait_ge(T.sem.sent, 8)
         return
@@ -82,18 +82,11 @@ def rank_program(g, core, T, topo):
         g.scalar.dma_start(T.y[:, W * rank:W * (rank + 1)], T.x[:]).then_inc(T.sem.stored, 16)
         n_st = 1
         for qn, q in (("sync", g.sync), ("scalar", g.scalar)):
-            for kind, r in STORES[qn]:
-                cols = slice(W * r, W * (r + 1))
-                b = T["b%d" % r]
-                if kind == "a":
-                    q.wait_ge(T.sem["a%d" % r], 8)
-                    q.dma_start(T.y[:, cols], b[:]).then_inc(T.sem.stored, 16)
-                elif kind == "m":
-                    q.wait_ge(T.sem["m%d" % r], expect["m%d" % r])
-                    q.dma_start(T.y[0:96, cols], b[0:3]).then_inc(T.sem.stored, 16)
-                else:
-                    q.wait_ge(T.sem["q%d" % r], expect["q%d" % r])
-                    q.dma_start(T.y[96:128, cols], b[3]).then_inc(T.sem.stored, 16)
+            for r, w in STORES[qn]:
+                name = "w%d_%d" % (r, w)
+                q.wait_ge(T.sem[name], expect[name])
+                q.dma_start(T.y[64 * w:64 * (w + 1), W * r:W * (r + 1)],
+                            T["b%d" % r][2 * w:2 * w + 2]).then_inc(T.sem.stored, 16)
                 n_st += 1
         g.wait_ge(T.sem.stored, 16 * n_st)
         return
@@ -101,15 +94,9 @@ def rank_program(g, core, T, topo):
     b = T["b%d" % rank]
     g.sync.dma_start(b[:], T.x[:]).then_inc(T.sem.loaded, 16)
     g.wait_ge(T.sem.loaded, 16)
-    if rank in WHOLE:
-        h = via(rank, WHOLE[rank])
-        if h is None:
-            g.remote_dma_fused([xfer(root, b[:], 0xFF, T.sem["a%d" % rank])], local_sem=T.sem.sent)
-            g.wait_ge(T.sem.sent, 8)
-        else:
-            g.remote_dma_fused([xfer(h, b[:], 0xFFFF, T.sem.hopin)], local_sem=T.sem.sent)
-            g.wait_ge(T.sem.sent, 16)
-    else:
-        fs = [first[(rank, s)] for s in range(4)]
-        g.remote_dma_fused([xfer(f[0], b[s], f[1], T.sem[f[3]]) for s, f in enumerate(fs)], local_sem=T.sem.sent)
-        g.wait_ge(T.sem.sent, sum(f[2] for f in fs))
+    total = 0
+    for w in (0, 1):
+        fs = [(s, first[(rank, s)]) for s in (2 * w, 2 * w + 1)]
+        g.remote_dma_fused([xfer(f[0], b[s], f[1], T.sem[f[3]]) for s, f in fs], local_sem=T.sem.sent)
+        total += sum(f[2] for _s, f in fs)
+    g.wait_ge(T.sem.sent, total)

from concourse.bass import DstId, RemoteDMATransfer

W = 256
A = ("A",)
WAYS = {
    0: [A, A, A, A],
    1: [A, A, A, A],
    2: [A, A, A, A],
    3: [("D", 4), ("D", 4), ("D", 5), ("D", 5)],
    4: [("D", 4), ("D", 4), ("D", 5), ("D", 5)],
    6: [("M", 3), ("M", 7), ("M", 2), ("M", 6)],
    7: [("M", 3), ("M", 7), ("M", 2), ("D", 4)],
}
STORES = {"sync": [(0, 0), (2, 0), (4, 0), (7, 0), (0, 1), (2, 1), (4, 1), (7, 1)],
          "scalar": [(1, 0), (3, 0), (6, 0), (1, 1), (3, 1), (6, 1)]}

SCRATCH = {}
for _r in WAYS:
    SCRATCH["b%d" % _r] = ("dram", [4, 128, 64], "float32")
SEMAPHORES = ["loaded", "sent", "hopin", "stored"] + ["w%d_%d" % (_r, _w) for _r in WAYS for _w in (0, 1)]


def rank_program(g, core, T, topo):
    root = T.cores[5]
    mate_chip = topo.chip(root) ^ 1

    def via(r, way):
        if way[0] == "A":
            return None
        return (topo.chip(T.cores[r]) if way[0] == "D" else mate_chip) * 8 + way[1]

    def xfer(dst, ap, mask, sem):
        rid, pid, _se = topo.addr(dst)
        return RemoteDMATransfer(dst_ids=[DstId(rid=rid, pnc=pid)], dma_engine_mask=mask, remote_sem=sem,
                                 src=ap, dst=ap)

    def bits(lo, n):
        return ((1 << n) - 1) << lo

    def wsem(r, s):
        return "w%d_%d" % (r, s // 2)

    first = {}
    holds = {}
    expect = {}
    for r, ways in WAYS.items():
        for w in (0, 1):
            both_on_chip = ways[2 * w][0] == "D" and ways[2 * w + 1][0] == "D"
            for j in (0, 1):
                s = 2 * w + j
                way = ways[s]
                h = via(r, way)
                if way[0] == "D":
                    mask, n = (bits(8 * j, 8) if both_on_chip else 0xFF00), 8
                else:
                    mask, n = bits(4 * j, 4), 4
                if h is None:
                    first[(r, s)] = (root, mask, n, wsem(r, s))
                    expect[wsem(r, s)] = expect.get(wsem(r, s), 0) + n
                else:
                    first[(r, s)] = (h, mask, n, "hopin")
                    holds.setdefault(h, []).append((r, s))
    for h, got in holds.items():
        for r, s in got:
            expect[wsem(r, s)] = expect.get(wsem(r, s), 0) + 8 // len(got)

    rank = T.rank_of(core)

    if core in holds:
        got = holds[core]
        g.wait_ge(T.sem.hopin, sum(first[k][2] for k in got))
        n = 8 // len(got)
        g.remote_dma_fused([xfer(root, T["b%d" % r][s], bits(n * j, n), T.sem[wsem(r, s)])
                            for j, (r, s) in enumerate(got)], local_sem=T.sem.sent)
        g.wait_ge(T.sem.sent, 8)
        return

    if rank is None:
        return

    if core == root:
        g.scalar.dma_start(T.y[:, W * rank:W * (rank + 1)], T.x[:]).then_inc(T.sem.stored, 16)
        n_st = 1
        for qn, q in (("sync", g.sync), ("scalar", g.scalar)):
            for r, w in STORES[qn]:
                name = "w%d_%d" % (r, w)
                q.wait_ge(T.sem[name], expect[name])
                q.dma_start(T.y[64 * w:64 * (w + 1), W * r:W * (r + 1)],
                            T["b%d" % r][2 * w:2 * w + 2]).then_inc(T.sem.stored, 16)
                n_st += 1
        g.wait_ge(T.sem.stored, 16 * n_st)
        return

    b = T["b%d" % rank]
    g.sync.dma_start(b[:], T.x[:]).then_inc(T.sem.loaded, 16)
    g.wait_ge(T.sem.loaded, 16)
    total = 0
    for w in (0, 1):
        fs = [(s, first[(rank, s)]) for s in (2 * w, 2 * w + 1)]
        g.remote_dma_fused([xfer(f[0], b[s], f[1], T.sem[f[3]]) for s, f in fs], local_sem=T.sem.sent)
        total += sum(f[2] for _s, f in fs)
    g.wait_ge(T.sem.sent, total)
